import numpy as np, ml_dtypes
CORES = [242,247,114,119]
N = 4
R, TK = 16, 512
def setup_inputs(rng):
    u = (rng.standard_normal((N, 128, R), dtype=np.float32) / 11).astype(ml_dtypes.bfloat16)
    return {"x": rng.standard_normal((N, 128, TK), dtype=np.float32).astype(ml_dtypes.bfloat16), "u": u, "ut": u.transpose(0, 2, 1).copy(), "vt": rng.standard_normal((N, R, 128), dtype=np.float32).astype(ml_dtypes.bfloat16)}
def setup_inputs_big(rng):
    d = setup_inputs(rng)
    for k in ("x", "u", "ut", "vt"): d[k] = (d[k].astype(np.float32) * 1024.0).astype(d[k].dtype)
    return d
def setup_inputs_small(rng):
    d = setup_inputs(rng)
    for k in ("x", "u", "ut", "vt"): d[k] = (d[k].astype(np.float32) * (1 / 1024.0)).astype(d[k].dtype)
    return d
def setup_inputs_apart(rng):
    d = setup_inputs(rng)
    f = (10.0 ** rng.permutation(np.linspace(-1.5, 1.5, N))).astype(np.float32).reshape(N, 1, 1)
    for k in ("x", "u", "ut", "vt"): d[k] = (d[k].astype(np.float32) * f).astype(d[k].dtype)
    return d
def reference(x, u, ut, vt):
    X, U, VT = x.astype(np.float64), u.astype(np.float64), vt.astype(np.float64)
    y = np.stack([sum(VT[j].T @ (U[j].T @ X[r]) for j in range(N)) for r in range(N)])
    return {"y": y.astype(ml_dtypes.bfloat16)}

@@ -1,0 +1,86 @@
+from concourse.bass import DstId, RemoteDMATransfer
+
+N, R, D, TK = 4, 16, 128, 512
+HALF = TK // 2
+
+SCRATCH = {
+    "fac": ("dram", [N, 128, 2 * R], "bfloat16"),
+    "f": ("sbuf", [128, 2 * D], "bfloat16"),
+    "xs": ("sbuf", [128, TK], "bfloat16"),
+    "wb": ("sbuf", [128, D], "bfloat16"),
+    "yb": ("sbuf", [128, TK], "bfloat16"),
+    "wp": ("psum", [128, 512], "float32"),
+    "ya": ("psum", [128, 512], "float32"),
+    "yc": ("psum", [128, 512], "float32"),
+}
+SEMAPHORES = ["staged", "xin", "near", "far", "sent", "laid", "w", "wb", "ya", "yc", "yb", "stored"]
+
+
+def _engines(mask):
+    return [e for e in range(mask.bit_length()) if (mask >> e) & 1]
+
+
+def rank_program(g, core, T, topo):
+    rank = T.rank_of(core)
+    if rank is None:
+        return
+    S, cores = T.sem, T.cores
+
+    def same_chip(a, b):
+        return topo.host(a) == topo.host(b) and topo.chip(a) == topo.chip(b)
+
+    home = [j for j in range(N) if same_chip(cores[j], core)]
+    away = [j for j in range(N) if j not in home]
+    for grp in (home, away):
+        assert grp == list(range(grp[0], grp[0] + len(grp)))
+    beside = [j for j in home if j != rank]
+
+    engine, off = {}, 0
+    for i, j in enumerate(away):
+        m = topo.mask(core, cores[j])
+        a = _engines(m)
+        engine[j] = a[i * len(a) // len(away)]
+        off |= m
+    for i, j in enumerate(beside):
+        a = _engines(topo.mask(core, cores[j]) & ~off)
+        engine[j] = a[i * len(a) // len(beside)]
+
+    g.sync.dma_start(T.fac[rank, 0:64, :], T.ut[:]).then_inc(S.staged, 16)
+    g.scalar.dma_start(T.fac[rank, 64:128, :], T.vt[:]).then_inc(S.staged, 16)
+    g.sync.dma_start(T.xs[:], T.x[:]).then_inc(S.xin, 16)
+
+    g.wait_ge(S.staged, 32)
+    transfers = []
+    for j in away + beside:
+        assert topo.may_write(core, cores[j])
+        rid, pid = topo.addr(cores[j], core)
+        transfers.append(RemoteDMATransfer(dst_ids=[DstId(rid=rid, pnc=pid)], dma_engine_mask=1 << engine[j],
+                                           remote_sem=S.far if j in away else S.near,
+                                           src=T.fac[rank], dst=T.fac[rank]))
+    g.remote_dma_fused(transfers, local_sem=S.sent)
+
+    for q, rows, cols in ((g.sync, slice(0, 64), slice(0, D)), (g.scalar, slice(64, 128), slice(D, 2 * D))):
+        q.wait_ge(S.staged, 32)
+        q.wait_ge(S.near, len(beside))
+        q.dma_start(T.f[R * home[0]:R * (home[-1] + 1), cols], T.fac[home[0]:home[-1] + 1, rows, :]).then_inc(S.laid, 16)
+        q.wait_ge(S.far, len(away))
+        q.dma_start(T.f[R * away[0]:R * (away[-1] + 1), cols], T.fac[away[0]:away[-1] + 1, rows, :]).then_inc(S.laid, 16)
+
+    g.tensor.wait_ge(S.laid, 64)
+    g.tensor.matmul(T.wp[:, 0:D], T.f[0:N * R, 0:D], T.f[0:N * R, D:2 * D], True, True).then_inc(S.w, 1)
+    g.vector.wait_ge(S.w, 1)
+    g.vector.tensor_copy(T.wb[:], T.wp[:, 0:D]).then_inc(S.wb, 1)
+
+    g.tensor.wait_ge(S.wb, 1)
+    g.tensor.wait_ge(S.xin, 16)
+    g.tensor.matmul(T.ya[:, 0:HALF], T.wb[:], T.xs[:, 0:HALF], True, True).then_inc(S.ya, 1)
+    g.tensor.matmul(T.yc[:, 0:HALF], T.wb[:], T.xs[:, HALF:TK], True, True).then_inc(S.yc, 1)
+    g.vector.wait_ge(S.ya, 1)
+    g.vector.tensor_copy(T.yb[:, 0:HALF], T.ya[:, 0:HALF]).then_inc(S.yb, 1)
+    g.vector.wait_ge(S.yc, 1)
+    g.vector.tensor_copy(T.yb[:, HALF:TK], T.yc[:, 0:HALF]).then_inc(S.yb, 1)
+
+    g.sync.wait_ge(S.yb, 2)
+    g.sync.dma_start(T.y[:], T.yb[:]).then_inc(S.stored, 16)
+    g.sync.wait_ge(S.stored, 16)
+    g.wait_ge(S.sent, len(transfers))

@@ -1,23 +1,25 @@
 from concourse.bass import DstId, RemoteDMATransfer
 
 N, R, D, TK = 4, 16, 128, 512
-HALF = TK // 2
+NB = 4
+BW = TK // NB
 
 SCRATCH = {
-    "fac": ("dram", [N, 128, 2 * R], "bfloat16"),
-    "f": ("sbuf", [128, 2 * D], "bfloat16"),
+    "a": ("sbuf", [128, 2 * D], "bfloat16"),
     "xs": ("sbuf", [128, TK], "bfloat16"),
-    "wb": ("sbuf", [128, D], "bfloat16"),
+    "wall": ("sbuf", [128, N * D], "bfloat16"),
     "yb": ("sbuf", [128, TK], "bfloat16"),
     "wp": ("psum", [128, 512], "float32"),
-    "ya": ("psum", [128, 512], "float32"),
-    "yc": ("psum", [128, 512], "float32"),
+    "y0": ("psum", [128, 512], "float32"),
+    "y1": ("psum", [128, 512], "float32"),
+    "y2": ("psum", [128, 512], "float32"),
+    "y3": ("psum", [128, 512], "float32"),
 }
-SEMAPHORES = ["staged", "xin", "near", "far", "sent", "laid", "w", "wb", "ya", "yc", "yb", "stored"]
+SEMAPHORES = ["loaded", "xin", "near", "early", "late", "sent", "w", "wb", "d0", "d1", "d2", "d3", "ylo", "yhi", "stored"]
 
 
-def _engines(mask):
-    return [e for e in range(mask.bit_length()) if (mask >> e) & 1]
+def _count(mask):
+    return sum((mask >> e) & 1 for e in range(mask.bit_length()))
 
 
 def rank_program(g, core, T, topo):
@@ -31,56 +33,59 @@ def rank_program(g, core, T, topo):
 
     home = [j for j in range(N) if same_chip(cores[j], core)]
     away = [j for j in range(N) if j not in home]
-    for grp in (home, away):
-        assert grp == list(range(grp[0], grp[0] + len(grp)))
-    beside = [j for j in home if j != rank]
+    assert len(home) == 2 and len(away) == 2
+    place = home.index(rank)
+    beside, first, second = home[1 - place], away[place], away[1 - place]
+    off = topo.mask(core, cores[first]) & topo.mask(core, cores[second])
+    on = topo.mask(core, cores[beside]) & ~off
+    n_off, n_on = _count(off), _count(on)
 
-    engine, off = {}, 0
-    for i, j in enumerate(away):
-        m = topo.mask(core, cores[j])
-        a = _engines(m)
-        engine[j] = a[i * len(a) // len(away)]
-        off |= m
-    for i, j in enumerate(beside):
-        a = _engines(topo.mask(core, cores[j]) & ~off)
-        engine[j] = a[i * len(a) // len(beside)]
+    def blk(j):
+        return T.wall[:, j * D:(j + 1) * D]
 
-    g.sync.dma_start(T.fac[rank, 0:64, :], T.ut[:]).then_inc(S.staged, 16)
-    g.scalar.dma_start(T.fac[rank, 64:128, :], T.vt[:]).then_inc(S.staged, 16)
-    g.sync.dma_start(T.xs[:], T.x[:]).then_inc(S.xin, 16)
-
-    g.wait_ge(S.staged, 32)
-    transfers = []
-    for j in away + beside:
+    def send(j, mask, sem):
         assert topo.may_write(core, cores[j])
         rid, pid = topo.addr(cores[j], core)
-        transfers.append(RemoteDMATransfer(dst_ids=[DstId(rid=rid, pnc=pid)], dma_engine_mask=1 << engine[j],
-                                           remote_sem=S.far if j in away else S.near,
-                                           src=T.fac[rank], dst=T.fac[rank]))
-    g.remote_dma_fused(transfers, local_sem=S.sent)
+        return RemoteDMATransfer(dst_ids=[DstId(rid=rid, pnc=pid)], dma_engine_mask=mask, remote_sem=sem,
+                                 src=blk(rank), dst=blk(rank))
 
-    for q, rows, cols in ((g.sync, slice(0, 64), slice(0, D)), (g.scalar, slice(64, 128), slice(D, 2 * D))):
-        q.wait_ge(S.staged, 32)
-        q.wait_ge(S.near, len(beside))
-        q.dma_start(T.f[R * home[0]:R * (home[-1] + 1), cols], T.fac[home[0]:home[-1] + 1, rows, :]).then_inc(S.laid, 16)
-        q.wait_ge(S.far, len(away))
-        q.dma_start(T.f[R * away[0]:R * (away[-1] + 1), cols], T.fac[away[0]:away[-1] + 1, rows, :]).then_inc(S.laid, 16)
+    g.sync.dma_start(T.a[0:R, 0:D], T.ut[:]).then_inc(S.loaded, 16)
+    g.scalar.dma_start(T.a[0:R, D:2 * D], T.vt[:]).then_inc(S.loaded, 16)
+    g.sync.dma_start(T.xs[:], T.x[:]).then_inc(S.xin, 16)
 
-    g.tensor.wait_ge(S.laid, 64)
-    g.tensor.matmul(T.wp[:, 0:D], T.f[0:N * R, 0:D], T.f[0:N * R, D:2 * D], True, True).then_inc(S.w, 1)
+    g.tensor.wait_ge(S.loaded, 32)
+    g.tensor.matmul(T.wp[:, 0:D], T.a[0:R, 0:D], T.a[0:R, D:2 * D], True, True).then_inc(S.w, 1)
     g.vector.wait_ge(S.w, 1)
-    g.vector.tensor_copy(T.wb[:], T.wp[:, 0:D]).then_inc(S.wb, 1)
+    g.vector.tensor_copy(blk(rank), T.wp[:, 0:D]).then_inc(S.wb, 1)
+
+    g.wait_ge(S.wb, 1)
+    g.remote_dma_fused([send(first, off, S.early)], local_sem=S.sent)
+    g.remote_dma_fused([send(second, off, S.late), send(beside, on, S.near)], local_sem=S.sent)
+
+    def acc(b, j, start, stop):
+        return g.tensor.matmul(T["y%d" % b][:, 0:BW], blk(j), T.xs[:, b * BW:(b + 1) * BW], start, stop)
 
     g.tensor.wait_ge(S.wb, 1)
     g.tensor.wait_ge(S.xin, 16)
-    g.tensor.matmul(T.ya[:, 0:HALF], T.wb[:], T.xs[:, 0:HALF], True, True).then_inc(S.ya, 1)
-    g.tensor.matmul(T.yc[:, 0:HALF], T.wb[:], T.xs[:, HALF:TK], True, True).then_inc(S.yc, 1)
-    g.vector.wait_ge(S.ya, 1)
-    g.vector.tensor_copy(T.yb[:, 0:HALF], T.ya[:, 0:HALF]).then_inc(S.yb, 1)
-    g.vector.wait_ge(S.yc, 1)
-    g.vector.tensor_copy(T.yb[:, HALF:TK], T.yc[:, 0:HALF]).then_inc(S.yb, 1)
+    for b in range(NB):
+        acc(b, rank, True, False)
+    g.tensor.wait_ge(S.near, n_on)
+    for b in range(NB):
+        acc(b, beside, False, False)
+    g.tensor.wait_ge(S.early, n_off)
+    for b in range(NB):
+        acc(b, first, False, False)
+    g.tensor.wait_ge(S.late, n_off)
+    for b in range(NB):
+        acc(b, second, False, True).then_inc(S["d%d" % b], 1)
+    for b in range(NB):
+        g.vector.wait_ge(S["d%d" % b], 1)
+        g.vector.tensor_copy(T.yb[:, b * BW:(b + 1) * BW], T["y%d" % b][:, 0:BW]).then_inc(S.ylo if b < NB // 2 else S.yhi, 1)
 
-    g.sync.wait_ge(S.yb, 2)
-    g.sync.dma_start(T.y[:], T.yb[:]).then_inc(S.stored, 16)
-    g.sync.wait_ge(S.stored, 16)
-    g.wait_ge(S.sent, len(transfers))
+    h = TK // 2
+    g.sync.wait_ge(S.ylo, NB // 2)
+    g.sync.dma_start(T.y[:, 0:h], T.yb[:, 0:h]).then_inc(S.stored, 16)
+    g.scalar.wait_ge(S.yhi, NB // 2)
+    g.scalar.dma_start(T.y[:, h:TK], T.yb[:, h:TK]).then_inc(S.stored, 16)
+    g.wait_ge(S.sent, 2 * n_off + n_on)
+    g.wait_ge(S.stored, 32)

@@ -6,16 +6,23 @@ BW = TK // NB
 
 SCRATCH = {
     "a": ("sbuf", [128, 2 * D], "bfloat16"),
+    "us": ("sbuf", [128, R], "bfloat16"),
+    "ub": ("sbuf", [128, R], "bfloat16"),
+    "z": ("sbuf", [128, D], "bfloat16"),
+    "zb": ("sbuf", [128, D], "bfloat16"),
+    "pb": ("sbuf", [128, TK], "bfloat16"),
     "xs": ("sbuf", [128, TK], "bfloat16"),
     "wall": ("sbuf", [128, N * D], "bfloat16"),
     "yb": ("sbuf", [128, TK], "bfloat16"),
     "wp": ("psum", [128, 512], "float32"),
+    "pp": ("psum", [128, 512], "float32"),
     "y0": ("psum", [128, 512], "float32"),
     "y1": ("psum", [128, 512], "float32"),
     "y2": ("psum", [128, 512], "float32"),
     "y3": ("psum", [128, 512], "float32"),
 }
-SEMAPHORES = ["loaded", "xin", "near", "early", "late", "sent", "w", "wb", "d0", "d1", "d2", "d3", "ylo", "yhi", "stored"]
+SEMAPHORES = ["pad", "uin", "zin", "loaded", "xin", "unear", "near", "early", "late", "sent", "w", "wb", "p", "pbs",
+              "d0", "d1", "d2", "d3", "ylo", "yhi", "stored"]
 
 
 def _count(mask):
@@ -43,15 +50,21 @@ def rank_program(g, core, T, topo):
     def blk(j):
         return T.wall[:, j * D:(j + 1) * D]
 
-    def send(j, mask, sem):
+    def send(j, mask, sem, src, dst):
         assert topo.may_write(core, cores[j])
         rid, pid = topo.addr(cores[j], core)
-        return RemoteDMATransfer(dst_ids=[DstId(rid=rid, pnc=pid)], dma_engine_mask=mask, remote_sem=sem,
-                                 src=blk(rank), dst=blk(rank))
+        return RemoteDMATransfer(dst_ids=[DstId(rid=rid, pnc=pid)], dma_engine_mask=mask, remote_sem=sem, src=src, dst=dst)
 
-    g.sync.dma_start(T.a[0:R, 0:D], T.ut[:]).then_inc(S.loaded, 16)
-    g.scalar.dma_start(T.a[0:R, D:2 * D], T.vt[:]).then_inc(S.loaded, 16)
+    g.vector.memset(T.z[:, :], 0.0).then_inc(S.pad, 1)
+    g.sync.dma_start(T.us[:], T.u[:]).then_inc(S.uin, 16)
+    g.scalar.dma_start(T.a[0:R, 0:D], T.ut[:]).then_inc(S.loaded, 16)
+    g.sync.dma_start(T.a[0:R, D:2 * D], T.vt[:]).then_inc(S.loaded, 16)
+    g.scalar.wait_ge(S.pad, 1)
+    g.scalar.dma_start(T.z[0:R, :], T.vt[:]).then_inc(S.zin, 16)
     g.sync.dma_start(T.xs[:], T.x[:]).then_inc(S.xin, 16)
+
+    g.wait_ge(S.uin, 16)
+    g.remote_dma_fused([send(beside, on, S.unear, T.us[:], T.ub[:])], local_sem=S.sent)
 
     g.tensor.wait_ge(S.loaded, 32)
     g.tensor.matmul(T.wp[:, 0:D], T.a[0:R, 0:D], T.a[0:R, D:2 * D], True, True).then_inc(S.w, 1)
@@ -59,8 +72,11 @@ def rank_program(g, core, T, topo):
     g.vector.tensor_copy(blk(rank), T.wp[:, 0:D]).then_inc(S.wb, 1)
 
     g.wait_ge(S.wb, 1)
-    g.remote_dma_fused([send(first, off, S.early)], local_sem=S.sent)
-    g.remote_dma_fused([send(second, off, S.late), send(beside, on, S.near)], local_sem=S.sent)
+    g.remote_dma_fused([send(first, off, S.early, blk(rank), blk(rank))], local_sem=S.sent)
+    g.wait_ge(S.pad, 1)
+    g.wait_ge(S.zin, 16)
+    g.remote_dma_fused([send(second, off, S.late, blk(rank), blk(rank)), send(beside, on, S.near, T.z[:], T.zb[:])],
+                       local_sem=S.sent)
 
     def acc(b, j, start, stop):
         return g.tensor.matmul(T["y%d" % b][:, 0:BW], blk(j), T.xs[:, b * BW:(b + 1) * BW], start, stop)
@@ -69,12 +85,17 @@ def rank_program(g, core, T, topo):
     g.tensor.wait_ge(S.xin, 16)
     for b in range(NB):
         acc(b, rank, True, False)
-    g.tensor.wait_ge(S.near, n_on)
-    for b in range(NB):
-        acc(b, beside, False, False)
+    g.tensor.wait_ge(S.unear, n_on)
+    g.tensor.matmul(T.pp[0:R, 0:TK], T.ub[:, 0:R], T.xs[:, 0:TK], True, True).then_inc(S.p, 1)
+    g.vector.wait_ge(S.p, 1)
+    g.vector.tensor_copy(T.pb[0:R, 0:TK], T.pp[0:R, 0:TK]).then_inc(S.pbs, 1)
     g.tensor.wait_ge(S.early, n_off)
     for b in range(NB):
         acc(b, first, False, False)
+    g.tensor.wait_ge(S.pbs, 1)
+    g.tensor.wait_ge(S.near, n_on)
+    for b in range(NB):
+        g.tensor.matmul(T["y%d" % b][:, 0:BW], T.zb[0:R, 0:D], T.pb[0:R, b * BW:(b + 1) * BW], False, False)
     g.tensor.wait_ge(S.late, n_off)
     for b in range(NB):
         acc(b, second, False, True).then_inc(S["d%d" % b], 1)
@@ -87,5 +108,5 @@ def rank_program(g, core, T, topo):
     g.sync.dma_start(T.y[:, 0:h], T.yb[:, 0:h]).then_inc(S.stored, 16)
     g.scalar.wait_ge(S.yhi, NB // 2)
     g.scalar.dma_start(T.y[:, h:TK], T.yb[:, h:TK]).then_inc(S.stored, 16)
-    g.wait_ge(S.sent, 2 * n_off + n_on)
+    g.wait_ge(S.sent, 2 * n_off + 2 * n_on)
     g.wait_ge(S.stored, 32)

@@ -6,7 +6,7 @@ BW = TK // NB
 
 SCRATCH = {
     "a": ("sbuf", [128, 2 * D], "bfloat16"),
-    "us": ("sbuf", [128, R], "bfloat16"),
+    "ud": ("dram", [128, R], "bfloat16"),
     "ub": ("sbuf", [128, R], "bfloat16"),
     "z": ("sbuf", [128, D], "bfloat16"),
     "zb": ("sbuf", [128, D], "bfloat16"),
@@ -15,14 +15,16 @@ SCRATCH = {
     "wall": ("sbuf", [128, N * D], "bfloat16"),
     "yb": ("sbuf", [128, TK], "bfloat16"),
     "wp": ("psum", [128, 512], "float32"),
-    "pp": ("psum", [128, 512], "float32"),
+    "pp0": ("psum", [128, 512], "float32"),
+    "pp1": ("psum", [128, 512], "float32"),
+    "pp2": ("psum", [128, 512], "float32"),
     "y0": ("psum", [128, 512], "float32"),
     "y1": ("psum", [128, 512], "float32"),
     "y2": ("psum", [128, 512], "float32"),
     "y3": ("psum", [128, 512], "float32"),
 }
-SEMAPHORES = ["pad", "uin", "zin", "loaded", "xin", "unear", "near", "early", "late", "sent", "w", "wb", "p", "pbs",
-              "d0", "d1", "d2", "d3", "ylo", "yhi", "stored"]
+SEMAPHORES = ["pad", "uin", "zin", "loaded", "xin", "unear", "near", "early", "late", "sent", "w", "wb",
+              "p0", "p1", "p2", "p3", "q0", "q1", "q2", "q3", "d0", "d1", "d2", "d3", "ylo", "yhi", "stored"]
 
 
 def _count(mask):
@@ -40,9 +42,11 @@ def rank_program(g, core, T, topo):
 
     home = [j for j in range(N) if same_chip(cores[j], core)]
     away = [j for j in range(N) if j not in home]
-    assert len(home) == 2 and len(away) == 2
-    place = home.index(rank)
-    beside, first, second = home[1 - place], away[place], away[1 - place]
+    across = [j for j in away if topo.die(cores[j]) != topo.die(core)]
+    straight = [j for j in away if topo.die(cores[j]) == topo.die(core)]
+    assert len(home) == 2 and len(across) == 1 and len(straight) == 1
+    beside = [j for j in home if j != rank][0]
+    first, second = straight[0], across[0]
     off = topo.mask(core, cores[first]) & topo.mask(core, cores[second])
     on = topo.mask(core, cores[beside]) & ~off
     n_off, n_on = _count(off), _count(on)
@@ -56,7 +60,7 @@ def rank_program(g, core, T, topo):
         return RemoteDMATransfer(dst_ids=[DstId(rid=rid, pnc=pid)], dma_engine_mask=mask, remote_sem=sem, src=src, dst=dst)
 
     g.vector.memset(T.z[:, :], 0.0).then_inc(S.pad, 1)
-    g.sync.dma_start(T.us[:], T.u[:]).then_inc(S.uin, 16)
+    g.sync.dma_start(T.ud[:], T.u[:]).then_inc(S.uin, 16)
     g.scalar.dma_start(T.a[0:R, 0:D], T.ut[:]).then_inc(S.loaded, 16)
     g.sync.dma_start(T.a[0:R, D:2 * D], T.vt[:]).then_inc(S.loaded, 16)
     g.scalar.wait_ge(S.pad, 1)
@@ -64,7 +68,7 @@ def rank_program(g, core, T, topo):
     g.sync.dma_start(T.xs[:], T.x[:]).then_inc(S.xin, 16)
 
     g.wait_ge(S.uin, 16)
-    g.remote_dma_fused([send(beside, on, S.unear, T.us[:], T.ub[:])], local_sem=S.sent)
+    g.remote_dma_fused([send(beside, off, S.unear, T.ud[:], T.ub[:])], local_sem=S.sent)
 
     g.tensor.wait_ge(S.loaded, 32)
     g.tensor.matmul(T.wp[:, 0:D], T.a[0:R, 0:D], T.a[0:R, D:2 * D], True, True).then_inc(S.w, 1)
@@ -85,16 +89,19 @@ def rank_program(g, core, T, topo):
     g.tensor.wait_ge(S.xin, 16)
     for b in range(NB):
         acc(b, rank, True, False)
-    g.tensor.wait_ge(S.unear, n_on)
-    g.tensor.matmul(T.pp[0:R, 0:TK], T.ub[:, 0:R], T.xs[:, 0:TK], True, True).then_inc(S.p, 1)
-    g.vector.wait_ge(S.p, 1)
-    g.vector.tensor_copy(T.pb[0:R, 0:TK], T.pp[0:R, 0:TK]).then_inc(S.pbs, 1)
+    g.tensor.wait_ge(S.unear, n_off)
+    pbank = [T.pp0, T.pp1, T.pp2, T.wp]
+    for b in range(NB):
+        g.tensor.matmul(pbank[b][0:R, 0:BW], T.ub[:, 0:R], T.xs[:, b * BW:(b + 1) * BW], True, True).then_inc(S["p%d" % b], 1)
+    for b in range(NB):
+        g.vector.wait_ge(S["p%d" % b], 1)
+        g.vector.tensor_copy(T.pb[0:R, b * BW:(b + 1) * BW], pbank[b][0:R, 0:BW]).then_inc(S["q%d" % b], 1)
     g.tensor.wait_ge(S.early, n_off)
     for b in range(NB):
         acc(b, first, False, False)
-    g.tensor.wait_ge(S.pbs, 1)
     g.tensor.wait_ge(S.near, n_on)
     for b in range(NB):
+        g.tensor.wait_ge(S["q%d" % b], 1)
         g.tensor.matmul(T["y%d" % b][:, 0:BW], T.zb[0:R, 0:D], T.pb[0:R, b * BW:(b + 1) * BW], False, False)
     g.tensor.wait_ge(S.late, n_off)
     for b in range(NB):
@@ -108,5 +115,5 @@ def rank_program(g, core, T, topo):
     g.sync.dma_start(T.y[:, 0:h], T.yb[:, 0:h]).then_inc(S.stored, 16)
     g.scalar.wait_ge(S.yhi, NB // 2)
     g.scalar.dma_start(T.y[:, h:TK], T.yb[:, h:TK]).then_inc(S.stored, 16)
-    g.wait_ge(S.sent, 2 * n_off + 2 * n_on)
+    g.wait_ge(S.sent, 3 * n_off + n_on)
     g.wait_ge(S.stored, 32)

from concourse.bass import DstId, RemoteDMATransfer

N, R, D, TK = 4, 16, 128, 512
NB = 4
BW = TK // NB

SCRATCH = {
    "a": ("sbuf", [128, 2 * D], "bfloat16"),
    "ud": ("dram", [128, R], "bfloat16"),
    "ub": ("sbuf", [128, R], "bfloat16"),
    "z": ("sbuf", [128, D], "bfloat16"),
    "zb": ("sbuf", [128, D], "bfloat16"),
    "pb": ("sbuf", [128, TK], "bfloat16"),
    "xs": ("sbuf", [128, TK], "bfloat16"),
    "wall": ("sbuf", [128, N * D], "bfloat16"),
    "yb": ("sbuf", [128, TK], "bfloat16"),
    "wp": ("psum", [128, 512], "float32"),
    "pp0": ("psum", [128, 512], "float32"),
    "pp1": ("psum", [128, 512], "float32"),
    "pp2": ("psum", [128, 512], "float32"),
    "y0": ("psum", [128, 512], "float32"),
    "y1": ("psum", [128, 512], "float32"),
    "y2": ("psum", [128, 512], "float32"),
    "y3": ("psum", [128, 512], "float32"),
}
SEMAPHORES = ["pad", "uin", "zin", "loaded", "xin", "unear", "near", "early", "late", "sent", "w", "wb",
              "p0", "p1", "p2", "p3", "q0", "q1", "q2", "q3", "d0", "d1", "d2", "d3", "ylo", "yhi", "stored"]


def _count(mask):
    return sum((mask >> e) & 1 for e in range(mask.bit_length()))


def rank_program(g, core, T, topo):
    rank = T.rank_of(core)
    if rank is None:
        return
    S, cores = T.sem, T.cores

    def same_chip(a, b):
        return topo.host(a) == topo.host(b) and topo.chip(a) == topo.chip(b)

    home = [j for j in range(N) if same_chip(cores[j], core)]
    away = [j for j in range(N) if j not in home]
    across = [j for j in away if topo.die(cores[j]) != topo.die(core)]
    straight = [j for j in away if topo.die(cores[j]) == topo.die(core)]
    assert len(home) == 2 and len(across) == 1 and len(straight) == 1
    beside = [j for j in home if j != rank][0]
    first, second = straight[0], across[0]
    off = topo.mask(core, cores[first]) & topo.mask(core, cores[second])
    on = topo.mask(core, cores[beside]) & ~off
    n_off, n_on = _count(off), _count(on)

    def blk(j):
        return T.wall[:, j * D:(j + 1) * D]

    def send(j, mask, sem, src, dst):
        assert topo.may_write(core, cores[j])
        rid, pid = topo.addr(cores[j], core)
        return RemoteDMATransfer(dst_ids=[DstId(rid=rid, pnc=pid)], dma_engine_mask=mask, remote_sem=sem, src=src, dst=dst)

    g.vector.memset(T.z[:, :], 0.0).then_inc(S.pad, 1)
    g.sync.dma_start(T.ud[:], T.u[:]).then_inc(S.uin, 16)
    g.scalar.dma_start(T.a[0:R, 0:D], T.ut[:]).then_inc(S.loaded, 16)
    g.sync.dma_start(T.a[0:R, D:2 * D], T.vt[:]).then_inc(S.loaded, 16)
    g.scalar.wait_ge(S.pad, 1)
    g.scalar.dma_start(T.z[0:R, :], T.vt[:]).then_inc(S.zin, 16)
    g.sync.dma_start(T.xs[:], T.x[:]).then_inc(S.xin, 16)

    g.wait_ge(S.uin, 16)
    g.remote_dma_fused([send(beside, off, S.unear, T.ud[:], T.ub[:])], local_sem=S.sent)

    g.tensor.wait_ge(S.loaded, 32)
    g.tensor.matmul(T.wp[:, 0:D], T.a[0:R, 0:D], T.a[0:R, D:2 * D], True, True).then_inc(S.w, 1)
    g.vector.wait_ge(S.w, 1)
    g.vector.tensor_copy(blk(rank), T.wp[:, 0:D]).then_inc(S.wb, 1)

    g.wait_ge(S.wb, 1)
    g.remote_dma_fused([send(first, off, S.early, blk(rank), blk(rank))], local_sem=S.sent)
    g.wait_ge(S.pad, 1)
    g.wait_ge(S.zin, 16)
    g.remote_dma_fused([send(second, off, S.late, blk(rank), blk(rank)), send(beside, on, S.near, T.z[:], T.zb[:])],
                       local_sem=S.sent)

    def acc(b, j, start, stop):
        return g.tensor.matmul(T["y%d" % b][:, 0:BW], blk(j), T.xs[:, b * BW:(b + 1) * BW], start, stop)

    g.tensor.wait_ge(S.wb, 1)
    g.tensor.wait_ge(S.xin, 16)
    for b in range(NB):
        acc(b, rank, True, False)
    g.tensor.wait_ge(S.unear, n_off)
    pbank = [T.pp0, T.pp1, T.pp2, T.wp]
    for b in range(NB):
        g.tensor.matmul(pbank[b][0:R, 0:BW], T.ub[:, 0:R], T.xs[:, b * BW:(b + 1) * BW], True, True).then_inc(S["p%d" % b], 1)
    for b in range(NB):
        g.vector.wait_ge(S["p%d" % b], 1)
        g.vector.tensor_copy(T.pb[0:R, b * BW:(b + 1) * BW], pbank[b][0:R, 0:BW]).then_inc(S["q%d" % b], 1)
    g.tensor.wait_ge(S.early, n_off)
    for b in range(NB):
        acc(b, first, False, False)
    g.tensor.wait_ge(S.near, n_on)
    for b in range(NB):
        g.tensor.wait_ge(S["q%d" % b], 1)
        g.tensor.matmul(T["y%d" % b][:, 0:BW], T.zb[0:R, 0:D], T.pb[0:R, b * BW:(b + 1) * BW], False, False)
    g.tensor.wait_ge(S.late, n_off)
    for b in range(NB):
        acc(b, second, False, True).then_inc(S["d%d" % b], 1)
    for b in range(NB):
        g.vector.wait_ge(S["d%d" % b], 1)
        g.vector.tensor_copy(T.yb[:, b * BW:(b + 1) * BW], T["y%d" % b][:, 0:BW]).then_inc(S.ylo if b < NB // 2 else S.yhi, 1)

    h = TK // 2
    g.sync.wait_ge(S.ylo, NB // 2)
    g.sync.dma_start(T.y[:, 0:h], T.yb[:, 0:h]).then_inc(S.stored, 16)
    g.scalar.wait_ge(S.yhi, NB // 2)
    g.scalar.dma_start(T.y[:, h:TK], T.yb[:, h:TK]).then_inc(S.stored, 16)
    g.wait_ge(S.sent, 3 * n_off + n_on)
    g.wait_ge(S.stored, 32)
